import numpy as np
import ml_dtypes


def mxq(x, axis, fmt="e4m3"):
    dtype, down = {"e4m3": (ml_dtypes.float8_e4m3fn, 7), "e5m2": (ml_dtypes.float8_e5m2, 14)}[fmt]
    v = np.moveaxis(np.asarray(x, np.float32).astype(ml_dtypes.bfloat16).astype(np.float64), axis, -1)
    blocks = v.reshape(v.shape[:-1] + (-1, 32))
    amax = np.abs(blocks).max(-1, keepdims=True)
    byte = np.maximum(np.where(amax > 0, np.frexp(amax)[1] - 1 + 127, 0) - down, 1)
    scale = np.exp2(byte - 127.0)
    codes = (blocks / scale).astype(np.float32).astype(dtype).astype(np.float64)
    return np.moveaxis((codes * scale).reshape(v.shape), -1, axis)


WIDE = False


def mx_kscale(k):
    if not WIDE:
        return np.ones(k)
    levels = np.array([10, -10, 5, -5, 0])
    if k % 512:
        return np.exp2(np.random.permutation(np.resize(levels, k // 32))).repeat(32)
    a = np.empty((k // 512, 16))
    for p in range(k // 512):
        a[p, :8] = np.random.permutation(np.resize(levels, 8))
        for g in range(8):
            far = levels[np.abs(levels - a[p, g]) >= 10]
            a[p, g + 8] = far[np.random.randint(len(far))]
    return np.exp2(a.ravel()).repeat(32)


def f64(x):
    return np.asarray(x).astype(np.float64)


def striped(idx):
    return np.tile(idx.reshape(-1, 16).T, (8, 1)).astype(np.uint16)


def unstriped(offs):
    return offs[:16].T.reshape(-1).astype(np.int64)


def striped8(idx):
    return np.concatenate([x.reshape(-1, 16).T for x in idx]).astype(np.uint16)


def runs(offs, k):
    lists = np.stack([offs[16 * r : 16 * r + 16].T.reshape(-1) for r in range(8)]).astype(np.int64)
    return lists[np.arange(k) % 512 // 64]


def pack_weight(w):
    k, n = w.shape
    w = f64(np.asarray(w, np.float32).astype(ml_dtypes.bfloat16)).reshape(k // 32, 32, n)
    amax = np.abs(w).max(1)
    byte = np.clip(np.where(amax > 0, np.frexp(amax)[1] - 1 + 127 - 7, 1), 1, 254)
    scaled = (w * np.exp2(127.0 - byte)[:, None, :]).reshape(k, n).astype(np.float32)
    words = np.ascontiguousarray(scaled.reshape(k // 512, 128, 4, n).transpose(0, 1, 3, 2)).astype(ml_dtypes.float8_e4m3fn).view(np.uint8)
    return words, np.ascontiguousarray(byte.astype(np.uint8).reshape(k // 512, 16, n))


def unpack_weight(words, scales):
    g, p, n, _ = words.shape
    vals = np.ascontiguousarray(words).view(ml_dtypes.float8_e4m3fn).astype(np.float64) * np.repeat(np.exp2(scales.astype(np.float64) - 127.0), 8, axis=1)[..., None]
    return vals.transpose(0, 1, 3, 2).reshape(g * 512, n)


def sigmoid(v):
    return 1.0 / (1.0 + np.exp(-np.maximum(v, -700.0)))

def planes(y):
    n, m = y.shape
    v = y.astype(np.float32).astype(ml_dtypes.bfloat16).astype(np.float64).reshape(n // 32, 32, m)
    top = np.abs(v).max(1)
    byte = np.clip(np.where(top > 0, np.frexp(top)[1] - 1 + 127 - 7, 1), 1, 254)
    codes = (v * np.exp2(127.0 - byte)[:, None, :]).reshape(n, m).astype(np.float32).astype(ml_dtypes.float8_e4m3fn).view(np.uint8)
    words = codes.reshape(n // 512, 128, 4, m).transpose(0, 1, 3, 2)
    return np.ascontiguousarray(words), np.ascontiguousarray(byte.astype(np.uint8).reshape(n // 512, 16, m))


K, T, S, G, H = 512, 2048, 512, 2048, 512


def setup_inputs():
    n = np.random.standard_normal
    s = mx_kscale(K)[:, None]
    packed_xT = pack_weight(n((K, T)) * s)
    packed_dT = pack_weight(n((K, G)) / s)
    return {
        "x_words": packed_xT[0],
        "x_scales": packed_xT[1],
        "d_words": packed_dT[0],
        "d_scales": packed_dT[1],
        "gs": (np.random.uniform(0.5, 1.5, (K, 1)) * s).astype(np.float32),
        "offs": striped(np.random.permutation(T)[:S]),
        "k1": striped8(np.random.randint(0, G, (8, H))),
        "n1": striped8(np.stack([np.random.permutation(S) for _ in range(8)])),
        "n2": striped8(np.stack([np.random.permutation(S) for _ in range(8)])),
        "n3": striped8(np.stack([np.random.permutation(S) for _ in range(8)])),
        "n4": striped8(np.stack([np.random.permutation(S) for _ in range(8)])),
        "n5": striped8(np.stack([np.random.permutation(S) for _ in range(8)])),
        "n6": striped8(np.stack([np.random.permutation(S) for _ in range(8)])),
    }


def reference(x_words, x_scales, d_words, d_scales, gs, offs, k1, n1, n2, n3, n4, n5, n6):
    d_k1 = unpack_weight(d_words, d_scales)[np.arange(K)[:, None], runs(k1, K)]
    xq = unpack_weight(x_words, x_scales)[:, unstriped(offs)]
    h = 0.0625 * (d_k1.T @ xq)
    z = f64(gs) * ((h[np.arange(H)[:, None], runs(n1, H)]) * sigmoid(h) + (h[np.arange(H)[:, None], runs(n2, H)]) * (sigmoid(h[np.arange(H)[:, None], runs(n3, H)])))
    h2 = 0.0625 * ((d_k1.T @ mxq(z, 0, "e4m3")))
    out_0 = 0.75 * (h2 * (h2[np.arange(H)[:, None], runs(n4, H)]) + (h2[np.arange(H)[:, None], runs(n5, H)]) * (h2[np.arange(H)[:, None], runs(n6, H)]))
    return (out_0,) + planes(out_0)

@@ -1,0 +1,208 @@
+import math
+from contextlib import ExitStack
+
+import concourse.mybir as mybir
+
+K, T, S, G, H = 512, 2048, 512, 2048, 512
+FLOPS = 2 * 2 * K * H * S
+
+F32 = mybir.dt.float32
+BF16 = mybir.dt.bfloat16
+I32 = mybir.dt.int32
+U32 = mybir.dt.uint32
+U16 = mybir.dt.uint16
+U8 = mybir.dt.uint8
+FP8X4 = mybir.dt.float8_e4m3fn_x4
+MULT = mybir.AluOpType.mult
+ADD = mybir.AluOpType.add
+COPY = mybir.ActivationFunctionType.Copy
+SIGMOID = mybir.ActivationFunctionType.Sigmoid
+
+P = 128
+PACK = 4
+LAST = PACK - 1
+WHOLE = (0, S)
+HALVES = ((0, 256), (256, 512))
+PIECES = ((0, 256), (256, 384), (384, 512))
+
+
+def entries(lst, a, b):
+    return lst[:, a // 16 : b // 16]
+
+
+def words_of(packed):
+    return packed[0].rearrange("p n t -> p (n t)").bitcast(I32)
+
+
+def tile_picked_ringwsumdot_none_po_kernel(
+    tc, x_words, x_scales, d_words, d_scales, gs, offs, k1, n1, n2, n3, n4, n5, n6, out_0, out_1, out_2
+):
+    nc = tc.nc
+    with ExitStack() as ctx:
+        keep = ctx.enter_context(tc.tile_pool(name="keep", bufs=1))
+        psum = ctx.enter_context(tc.psum_pool(name="psum", bufs=8))
+
+        def sb(name, shape, dtype):
+            return keep.tile(shape, dtype, name=name, align_bytes=64)
+
+        def load_list(name, src):
+            lst = sb(name, [P, S // 16], U16)
+            nc.sync.dma_start(lst[:], src)
+            return lst
+
+        d_byte_table = sb("d_byte_table", [P, G], U8)
+        x_byte_table = sb("x_byte_table", [P, T], U8)
+        d_word_table = sb("d_word_table", [P, G], I32)
+        x_word_table = sb("x_word_table", [P, T], I32)
+        nc.gpsimd.memset(d_byte_table[:].bitcast(I32), 0)
+        nc.vector.memset(x_byte_table[:].bitcast(I32), 0)
+        k1_sb = load_list("k1_sb", k1)
+        offs_sb = load_list("offs_sb", offs)
+        nc.sync.dma_start(d_word_table[:], words_of(d_words))
+        nc.scalar.dma_start(d_byte_table[0:P:8, :].bitcast(I32), d_scales[0].bitcast(I32))
+        nc.scalar.dma_start(x_byte_table[0:P:8, :].bitcast(I32), x_scales[0].bitcast(I32))
+        nc.sync.dma_start(x_word_table[:], words_of(x_words))
+        gs_sb = sb("gs_sb", [P, PACK], F32)
+        nc.sync.dma_start(gs_sb[:], gs.rearrange("(p t) o -> p (t o)", t=PACK))
+        n1_sb = load_list("n1_sb", n1)
+        n3_sb = load_list("n3_sb", n3)
+        n2_sb = load_list("n2_sb", n2)
+        n5_sb = load_list("n5_sb", n5)
+        n4_sb = load_list("n4_sb", n4)
+        n6_sb = load_list("n6_sb", n6)
+
+        scales = sb("scales", [P, H + S], U8)
+        nc.vector.memset(scales[:].bitcast(I32), 0)
+
+        rows = [sb("rows%d" % t, [P, S if t == LAST else 2 * S], F32) for t in range(PACK)]
+        gained = [sb("gained%d" % t, [P, S if t == LAST else 2 * S], F32) for t in range(PACK)]
+        for t in range(LAST):
+            nc.gpsimd.memset(gained[t][:, S:], 0.0)
+            nc.gpsimd.memset(rows[t][:, S:], 0.0)
+
+        warm = sb("warm", [P, 1], F32)
+        nc.scalar.activation(warm[:], gained[0][:, S : S + 1], SIGMOID)
+        gs16 = sb("gs16", [P, 1], F32)
+        nc.scalar.activation(gs16[:], gs_sb[:, 0:1], COPY, scale=0.0625)
+
+        d_bytes = sb("d_bytes", [P, H], U8)
+        x_bytes = sb("x_bytes", [P, S], U8)
+        spread = sb("spread", [P, H + S], U8)
+        nc.vector.tensor_copy(d_bytes[:], d_byte_table[:].indirect(k1_sb[:]))
+        nc.vector.tensor_copy(x_bytes[:], x_byte_table[:].indirect(offs_sb[:]))
+        nc.vector.tensor_copy(
+            spread[:, :H].rearrange("p (t m) -> p m t", t=PACK), d_bytes[:].rearrange("p (m t) -> p m t", t=PACK)
+        )
+        nc.vector.tensor_copy(spread[:, H:].bitcast(I32), x_bytes[:].bitcast(I32))
+        for j in range(PACK):
+            nc.scalar.dma_start(scales[j:P:32, :].bitcast(I32), spread[8 * j : P : 32, :].bitcast(I32))
+
+        d_picked = sb("d_picked", [P, H], U32)
+        d_codes = sb("d_codes", [P, H], U32)
+        x_codes = sb("x_codes", [P, S], U32)
+        nc.vector.tensor_copy(d_picked[:], d_word_table[:].bitcast(U32).indirect(k1_sb[:]))
+        nc.vector.tensor_copy(
+            d_codes[:].bitcast(I32).rearrange("p (t m) -> p m t", t=PACK),
+            d_picked[:].bitcast(I32).rearrange("p (m t) -> p m t", t=PACK),
+        )
+        for a, b in HALVES:
+            nc.vector.tensor_copy(x_codes[:, a:b], x_word_table[:].bitcast(U32).indirect(entries(offs_sb, a, b)))
+
+        def product(out, t, codes, codes_scale):
+            nc.tensor.matmul_mx(
+                out,
+                lhsT=d_codes[:, t * P : (t + 1) * P].bitcast(FP8X4),
+                lhsT_scale=scales[:, t * P : (t + 1) * P],
+                rhs=codes.bitcast(FP8X4),
+                rhs_scale=codes_scale,
+                start=True,
+                stop=True,
+            )
+
+        sig = sb("sig", [P, PACK, S], F32)
+        sig3 = sb("sig3", [P, PACK, S], F32)
+        left = sb("left", [P, PACK, S], F32)
+        right = sb("right", [P, PACK, S], F32)
+        z_bf = sb("z_bf", [P, S * PACK], BF16)
+        z_codes = sb("z_codes", [P, S], U32)
+        z_scales = sb("z_scales", [P, S], U8)
+
+        for t in range(PACK):
+            spans = HALVES if t == 0 else (WHOLE,)
+            banks = []
+            for a, b in spans:
+                bank = psum.tile([P, S], F32, name="bank")
+                product(bank[:, : b - a], t, x_codes[:, a:b], scales[:, H + a : H + b])
+                banks.append(bank)
+            for (a, b), bank in zip(spans, banks):
+                if t == 0:
+                    nc.scalar.activation(gained[t][:, a:b], bank[:, : b - a], COPY, scale=gs16[:])
+                else:
+                    nc.scalar.activation(rows[t][:, a:b], bank[:, : b - a], COPY, scale=0.0625)
+                nc.scalar.activation(sig[:, t, a:b], bank[:, : b - a], SIGMOID, scale=0.0625)
+            if t == 0:
+                for (a, b), bank in zip(spans, banks):
+                    nc.scalar.activation(rows[t][:, a:b], bank[:, : b - a], COPY, scale=0.0625)
+            else:
+                nc.vector.tensor_scalar(gained[t][:, :S], rows[t][:, :S], gs_sb[:, t : t + 1], None, MULT)
+            for a, b in HALVES if t == LAST else (WHOLE,):
+                nc.scalar.activation(sig3[:, t, a:b], rows[t][:].indirect(entries(n3_sb, a, b)), SIGMOID)
+            for a, b in PIECES if t == LAST else (WHOLE,):
+                nc.vector.tensor_tensor(left[:, t, a:b], gained[t][:].indirect(entries(n1_sb, a, b)), sig[:, t, a:b], MULT)
+                nc.vector.tensor_tensor(right[:, t, a:b], gained[t][:].indirect(entries(n2_sb, a, b)), sig3[:, t, a:b], MULT)
+                if t == LAST:
+                    nc.vector.tensor_tensor(
+                        z_bf[:, PACK * a : PACK * b].rearrange("p (c i t) -> p c t i", i=4, t=PACK),
+                        left[:, :, a:b].rearrange("p t (c i) -> p c t i", i=4),
+                        right[:, :, a:b].rearrange("p t (c i) -> p c t i", i=4),
+                        ADD,
+                    )
+                    nc.vector.quantize_mx(z_codes[:, a:b].bitcast(FP8X4), z_scales[:, a:b], z_bf[:, PACK * a : PACK * b])
+
+        root = 0.0625 * math.sqrt(0.75)
+        plain = sb("plain", [P, PACK, S], F32)
+        at5 = sb("at5", [P, PACK, S], F32)
+        term4 = sb("term4", [P, PACK, S], F32)
+        term56 = sb("term56", [P, PACK, S], F32)
+        y = sb("y", [P, PACK, S], F32)
+        y_bf = sb("y_bf", [P, S * PACK], BF16)
+        y_codes = sb("y_codes", [P, S], U32)
+        y_scales = sb("y_scales", [P, S], U8)
+        out_rows = out_0.rearrange("(p t) n -> p t n", t=PACK)
+        out_words = words_of(out_1)
+
+        for t in range(PACK):
+            if t == 0:
+                early = psum.tile([P, S], F32, name="bank")
+                late = psum.tile([P, S], F32, name="bank")
+                for a, b in PIECES[:-1]:
+                    product(early[:, a:b], t, z_codes[:, a:b], z_scales[:, a:b])
+                a, b = PIECES[-1]
+                product(late[:, a:b], t, z_codes[:, a:b], z_scales[:, a:b])
+                parts = ((0, a, early), (a, b, late))
+            else:
+                bank = psum.tile([P, S], F32, name="bank")
+                product(bank[:], t, z_codes[:], z_scales[:])
+                parts = ((0, S, bank),)
+            for a, b, src in parts:
+                nc.scalar.activation(rows[t][:, a:b], src[:, a:b], COPY, scale=root)
+            for a, b, src in parts:
+                nc.scalar.activation(plain[:, t, a:b], src[:, a:b], COPY, scale=root)
+            for a, b in PIECES if t == LAST else (WHOLE,):
+                nc.vector.tensor_copy(at5[:, t, a:b], rows[t][:].indirect(entries(n5_sb, a, b)))
+                nc.vector.tensor_tensor(term4[:, t, a:b], rows[t][:].indirect(entries(n4_sb, a, b)), plain[:, t, a:b], MULT)
+                nc.vector.tensor_tensor(term56[:, t, a:b], rows[t][:].indirect(entries(n6_sb, a, b)), at5[:, t, a:b], MULT)
+                nc.vector.tensor_tensor(y[:, t, a:b], term4[:, t, a:b], term56[:, t, a:b], ADD)
+                nc.sync.dma_start(out_rows[:, t, a:b], y[:, t, a:b])
+                if t == LAST:
+                    woven = y_bf[:, PACK * a : PACK * b].rearrange("p (c i t) -> p c t i", i=4, t=PACK)
+                    planes = y[:, :, a:b].rearrange("p t (c i) -> p c t i", i=4)
+                    if b == S:
+                        nc.vector.tensor_copy(woven, planes)
+                    else:
+                        nc.scalar.copy(woven, planes)
+                    nc.vector.quantize_mx(y_codes[:, a:b].bitcast(FP8X4), y_scales[:, a:b], y_bf[:, PACK * a : PACK * b])
+                    nc.scalar.dma_start(out_words[:, a:b], y_codes[:, a:b].bitcast(I32))
+        for q in range(4):
+            queue = nc.sync if q % 2 == 0 else nc.scalar
+            queue.dma_start(out_2[0, 4 * q : 4 * q + 4, :].bitcast(I32), y_scales[32 * q : 32 * q + 4, :].bitcast(I32))

@@ -2,6 +2,7 @@ import math
 from contextlib import ExitStack
 
 import concourse.mybir as mybir
+from concourse.masks import make_identity
 
 K, T, S, G, H = 512, 2048, 512, 2048, 512
 FLOPS = 2 * 2 * K * H * S
@@ -21,6 +22,7 @@ SIGMOID = mybir.ActivationFunctionType.Sigmoid
 P = 128
 PACK = 4
 LAST = PACK - 1
+FIRST = 512
 WHOLE = (0, S)
 HALVES = ((0, 256), (256, 512))
 PIECES = ((0, 256), (256, 384), (384, 512))
@@ -57,10 +59,11 @@ def tile_picked_ringwsumdot_none_po_kernel(
         nc.gpsimd.memset(d_byte_table[:].bitcast(I32), 0)
         nc.vector.memset(x_byte_table[:].bitcast(I32), 0)
         k1_sb = load_list("k1_sb", k1)
+        nc.sync.dma_start(d_word_table[:, :FIRST], words_of(d_words)[:, :FIRST])
+        nc.sync.dma_start(d_byte_table[0:P:8, :].bitcast(I32), d_scales[0].bitcast(I32))
         offs_sb = load_list("offs_sb", offs)
-        nc.sync.dma_start(d_word_table[:], words_of(d_words))
-        nc.scalar.dma_start(d_byte_table[0:P:8, :].bitcast(I32), d_scales[0].bitcast(I32))
-        nc.scalar.dma_start(x_byte_table[0:P:8, :].bitcast(I32), x_scales[0].bitcast(I32))
+        nc.sync.dma_start(x_byte_table[0:P:8, :].bitcast(I32), x_scales[0].bitcast(I32))
+        nc.sync.dma_start(d_word_table[:, FIRST:], words_of(d_words)[:, FIRST:])
         nc.sync.dma_start(x_word_table[:], words_of(x_words))
         gs_sb = sb("gs_sb", [P, PACK], F32)
         nc.sync.dma_start(gs_sb[:], gs.rearrange("(p t) o -> p (t o)", t=PACK))
@@ -80,10 +83,10 @@ def tile_picked_ringwsumdot_none_po_kernel(
             nc.gpsimd.memset(gained[t][:, S:], 0.0)
             nc.gpsimd.memset(rows[t][:, S:], 0.0)
 
+        ident = sb("ident", [P, P], F32)
+        make_identity(nc, ident[:])
         warm = sb("warm", [P, 1], F32)
         nc.scalar.activation(warm[:], gained[0][:, S : S + 1], SIGMOID)
-        gs16 = sb("gs16", [P, 1], F32)
-        nc.scalar.activation(gs16[:], gs_sb[:, 0:1], COPY, scale=0.0625)
 
         d_bytes = sb("d_bytes", [P, H], U8)
         x_bytes = sb("x_bytes", [P, S], U8)
@@ -127,37 +130,45 @@ def tile_picked_ringwsumdot_none_po_kernel(
         z_codes = sb("z_codes", [P, S], U32)
         z_scales = sb("z_scales", [P, S], U8)
 
+        def weave(dst, a, b, i):
+            return dst[:, PACK * a : PACK * b].rearrange("p (c i t) -> p c t i", i=i, t=PACK)
+
+        def planes(src, a, b, i):
+            return src[:, :, a:b].rearrange("p t (c i) -> p c t i", i=i)
+
+        def first_term(t, a, b):
+            nc.vector.tensor_tensor(left[:, t, a:b], gained[t][:].indirect(entries(n1_sb, a, b)), sig[:, t, a:b], MULT)
+
+        def second_term(t, a, b):
+            nc.vector.tensor_tensor(right[:, t, a:b], gained[t][:].indirect(entries(n2_sb, a, b)), sig3[:, t, a:b], MULT)
+
+        def sum_z(a, b):
+            nc.vector.tensor_tensor(weave(z_bf, a, b, 4), planes(left, a, b, 4), planes(right, a, b, 4), ADD)
+
+        def quantise_z(a, b):
+            nc.vector.quantize_mx(z_codes[:, a:b].bitcast(FP8X4), z_scales[:, a:b], z_bf[:, PACK * a : PACK * b])
+
         for t in range(PACK):
-            spans = HALVES if t == 0 else (WHOLE,)
-            banks = []
-            for a, b in spans:
+            for a, b in HALVES if t == 0 else (WHOLE,):
                 bank = psum.tile([P, S], F32, name="bank")
                 product(bank[:, : b - a], t, x_codes[:, a:b], scales[:, H + a : H + b])
-                banks.append(bank)
-            for (a, b), bank in zip(spans, banks):
-                if t == 0:
-                    nc.scalar.activation(gained[t][:, a:b], bank[:, : b - a], COPY, scale=gs16[:])
-                else:
-                    nc.scalar.activation(rows[t][:, a:b], bank[:, : b - a], COPY, scale=0.0625)
+                nc.scalar.activation(rows[t][:, a:b], bank[:, : b - a], COPY, scale=0.0625)
                 nc.scalar.activation(sig[:, t, a:b], bank[:, : b - a], SIGMOID, scale=0.0625)
-            if t == 0:
-                for (a, b), bank in zip(spans, banks):
-                    nc.scalar.activation(rows[t][:, a:b], bank[:, : b - a], COPY, scale=0.0625)
-            else:
-                nc.vector.tensor_scalar(gained[t][:, :S], rows[t][:, :S], gs_sb[:, t : t + 1], None, MULT)
+                nc.vector.tensor_scalar(gained[t][:, a:b], rows[t][:, a:b], gs_sb[:, t : t + 1], None, MULT)
             for a, b in HALVES if t == LAST else (WHOLE,):
                 nc.scalar.activation(sig3[:, t, a:b], rows[t][:].indirect(entries(n3_sb, a, b)), SIGMOID)
-            for a, b in PIECES if t == LAST else (WHOLE,):
-                nc.vector.tensor_tensor(left[:, t, a:b], gained[t][:].indirect(entries(n1_sb, a, b)), sig[:, t, a:b], MULT)
-                nc.vector.tensor_tensor(right[:, t, a:b], gained[t][:].indirect(entries(n2_sb, a, b)), sig3[:, t, a:b], MULT)
-                if t == LAST:
-                    nc.vector.tensor_tensor(
-                        z_bf[:, PACK * a : PACK * b].rearrange("p (c i t) -> p c t i", i=4, t=PACK),
-                        left[:, :, a:b].rearrange("p t (c i) -> p c t i", i=4),
-                        right[:, :, a:b].rearrange("p t (c i) -> p c t i", i=4),
-                        ADD,
-                    )
-                    nc.vector.quantize_mx(z_codes[:, a:b].bitcast(FP8X4), z_scales[:, a:b], z_bf[:, PACK * a : PACK * b])
+            if t < LAST:
+                first_term(t, *WHOLE)
+                second_term(t, *WHOLE)
+        lo, hi = HALVES
+        first_term(LAST, *lo)
+        second_term(LAST, *lo)
+        first_term(LAST, *hi)
+        sum_z(*lo)
+        second_term(LAST, *hi)
+        quantise_z(*lo)
+        sum_z(*hi)
+        quantise_z(*hi)
 
         root = 0.0625 * math.sqrt(0.75)
         plain = sb("plain", [P, PACK, S], F32)
@@ -165,44 +176,72 @@ def tile_picked_ringwsumdot_none_po_kernel(
         term4 = sb("term4", [P, PACK, S], F32)
         term56 = sb("term56", [P, PACK, S], F32)
         y = sb("y", [P, PACK, S], F32)
+        y_turned = sb("y_turned", [P, 2, S], F32)
         y_bf = sb("y_bf", [P, S * PACK], BF16)
         y_codes = sb("y_codes", [P, S], U32)
         y_scales = sb("y_scales", [P, S], U8)
         out_rows = out_0.rearrange("(p t) n -> p t n", t=PACK)
         out_words = words_of(out_1)
 
+        def fetch5(t, a, b):
+            nc.vector.tensor_copy(at5[:, t, a:b], rows[t][:].indirect(entries(n5_sb, a, b)))
+
+        def terms(t, a, b):
+            nc.vector.tensor_tensor(term4[:, t, a:b], rows[t][:].indirect(entries(n4_sb, a, b)), plain[:, t, a:b], MULT)
+            nc.vector.tensor_tensor(term56[:, t, a:b], rows[t][:].indirect(entries(n6_sb, a, b)), at5[:, t, a:b], MULT)
+
+        def sum_y(t, a, b):
+            nc.vector.tensor_tensor(y[:, t, a:b], term4[:, t, a:b], term56[:, t, a:b], ADD)
+            nc.sync.dma_start(out_rows[:, t, a:b], y[:, t, a:b])
+
+        def sum_y_by_transposes(t):
+            turned = psum.tile([P, S], F32, name="bank")
+            for c in range(0, S, P):
+                for src, first in ((term4, True), (term56, False)):
+                    nc.tensor.matmul(
+                        turned[:, c : c + P], lhsT=src[:, t, c : c + P], rhs=ident[:], is_transpose=True, start=first, stop=not first
+                    )
+            nc.scalar.copy(y_turned[:, t, :], turned[:])
+            back = psum.tile([P, S], F32, name="bank")
+            for c in range(0, S, P):
+                nc.tensor.transpose(back[:, c : c + P], y_turned[:, t, c : c + P], ident[:])
+            nc.scalar.copy(y[:, t, :], back[:])
+            nc.scalar.dma_start(out_rows[:, t, :], y[:, t, :])
+
+        def quantise_y(a, b, queue):
+            nc.vector.quantize_mx(y_codes[:, a:b].bitcast(FP8X4), y_scales[:, a:b], y_bf[:, PACK * a : PACK * b])
+            queue.dma_start(out_words[:, a:b], y_codes[:, a:b].bitcast(I32))
+
         for t in range(PACK):
-            if t == 0:
-                early = psum.tile([P, S], F32, name="bank")
-                late = psum.tile([P, S], F32, name="bank")
-                for a, b in PIECES[:-1]:
-                    product(early[:, a:b], t, z_codes[:, a:b], z_scales[:, a:b])
-                a, b = PIECES[-1]
-                product(late[:, a:b], t, z_codes[:, a:b], z_scales[:, a:b])
-                parts = ((0, a, early), (a, b, late))
-            else:
+            banks = []
+            for a, b in HALVES if t == 0 else (WHOLE,):
                 bank = psum.tile([P, S], F32, name="bank")
-                product(bank[:], t, z_codes[:], z_scales[:])
-                parts = ((0, S, bank),)
-            for a, b, src in parts:
-                nc.scalar.activation(rows[t][:, a:b], src[:, a:b], COPY, scale=root)
-            for a, b, src in parts:
-                nc.scalar.activation(plain[:, t, a:b], src[:, a:b], COPY, scale=root)
-            for a, b in PIECES if t == LAST else (WHOLE,):
-                nc.vector.tensor_copy(at5[:, t, a:b], rows[t][:].indirect(entries(n5_sb, a, b)))
-                nc.vector.tensor_tensor(term4[:, t, a:b], rows[t][:].indirect(entries(n4_sb, a, b)), plain[:, t, a:b], MULT)
-                nc.vector.tensor_tensor(term56[:, t, a:b], rows[t][:].indirect(entries(n6_sb, a, b)), at5[:, t, a:b], MULT)
-                nc.vector.tensor_tensor(y[:, t, a:b], term4[:, t, a:b], term56[:, t, a:b], ADD)
-                nc.sync.dma_start(out_rows[:, t, a:b], y[:, t, a:b])
-                if t == LAST:
-                    woven = y_bf[:, PACK * a : PACK * b].rearrange("p (c i t) -> p c t i", i=4, t=PACK)
-                    planes = y[:, :, a:b].rearrange("p t (c i) -> p c t i", i=4)
-                    if b == S:
-                        nc.vector.tensor_copy(woven, planes)
-                    else:
-                        nc.scalar.copy(woven, planes)
-                    nc.vector.quantize_mx(y_codes[:, a:b].bitcast(FP8X4), y_scales[:, a:b], y_bf[:, PACK * a : PACK * b])
-                    nc.scalar.dma_start(out_words[:, a:b], y_codes[:, a:b].bitcast(I32))
+                product(bank[:, a:b], t, z_codes[:, a:b], z_scales[:, a:b])
+                nc.scalar.activation(rows[t][:, a:b], bank[:, a:b], COPY, scale=root)
+                banks.append((a, b, bank))
+            for a, b, bank in banks:
+                nc.scalar.activation(plain[:, t, a:b], bank[:, a:b], COPY, scale=root)
+            if t < LAST:
+                fetch5(t, *WHOLE)
+                terms(t, *WHOLE)
+        for t in range(2):
+            sum_y_by_transposes(t)
+        one, two, three = PIECES
+        fetch5(LAST, *one)
+        sum_y(LAST - 1, *WHOLE)
+        terms(LAST, *one)
+        fetch5(LAST, *two)
+        sum_y(LAST, *one)
+        nc.scalar.copy(weave(y_bf, *one, 4), planes(y, *one, 4))
+        terms(LAST, *two)
+        fetch5(LAST, *three)
+        sum_y(LAST, *two)
+        nc.scalar.copy(weave(y_bf, *two, 4), planes(y, *two, 4))
+        terms(LAST, *three)
+        nc.vector.tensor_tensor(weave(y_bf, *three, 4), planes(term4, *three, 4), planes(term56, *three, 4), ADD)
+        sum_y(LAST, *three)
+        quantise_y(*lo, nc.sync)
+        quantise_y(*hi, nc.scalar)
         for q in range(4):
-            queue = nc.sync if q % 2 == 0 else nc.scalar
+            queue = nc.sync if q < 2 else nc.scalar
             queue.dma_start(out_2[0, 4 * q : 4 * q + 4, :].bitcast(I32), y_scales[32 * q : 32 * q + 4, :].bitcast(I32))

@@ -79,14 +79,11 @@ def tile_picked_ringwsumdot_none_po_kernel(
 
         rows = [sb("rows%d" % t, [P, S if t == LAST else 2 * S], F32) for t in range(PACK)]
         gained = [sb("gained%d" % t, [P, S if t == LAST else 2 * S], F32) for t in range(PACK)]
-        for t in range(LAST):
-            nc.gpsimd.memset(gained[t][:, S:], 0.0)
-            nc.gpsimd.memset(rows[t][:, S:], 0.0)
 
         ident = sb("ident", [P, P], F32)
         make_identity(nc, ident[:])
-        warm = sb("warm", [P, 1], F32)
-        nc.scalar.activation(warm[:], gained[0][:, S : S + 1], SIGMOID)
+        zero = sb("zero", [P, 1], F32)
+        nc.vector.memset(zero[:], 0.0)
 
         d_bytes = sb("d_bytes", [P, H], U8)
         x_bytes = sb("x_bytes", [P, S], U8)
@@ -94,19 +91,23 @@ def tile_picked_ringwsumdot_none_po_kernel(
         nc.vector.tensor_copy(d_bytes[:], d_byte_table[:].indirect(k1_sb[:]))
         nc.vector.tensor_copy(x_bytes[:], x_byte_table[:].indirect(offs_sb[:]))
         nc.vector.tensor_copy(
-            spread[:, :H].rearrange("p (t m) -> p m t", t=PACK), d_bytes[:].rearrange("p (m t) -> p m t", t=PACK)
+            spread[:, :H].rearrange("p (t m) -> p t m", t=PACK), d_bytes[:].rearrange("p (m t) -> p t m", t=PACK)
         )
         nc.vector.tensor_copy(spread[:, H:].bitcast(I32), x_bytes[:].bitcast(I32))
         for j in range(PACK):
             nc.scalar.dma_start(scales[j:P:32, :].bitcast(I32), spread[8 * j : P : 32, :].bitcast(I32))
+
+        for t in range(LAST):
+            for window in (gained[t], rows[t]):
+                nc.scalar.activation(window[:, S:], zero[:].to_broadcast([P, S]), SIGMOID)
 
         d_picked = sb("d_picked", [P, H], U32)
         d_codes = sb("d_codes", [P, H], U32)
         x_codes = sb("x_codes", [P, S], U32)
         nc.vector.tensor_copy(d_picked[:], d_word_table[:].bitcast(U32).indirect(k1_sb[:]))
         nc.vector.tensor_copy(
-            d_codes[:].bitcast(I32).rearrange("p (t m) -> p m t", t=PACK),
-            d_picked[:].bitcast(I32).rearrange("p (m t) -> p m t", t=PACK),
+            d_codes[:].bitcast(I32).rearrange("p (t c i) -> p c t i", t=PACK, i=4),
+            d_picked[:].bitcast(I32).rearrange("p (c i t) -> p c t i", t=PACK, i=4),
         )
         for a, b in HALVES:
             nc.vector.tensor_copy(x_codes[:, a:b], x_word_table[:].bitcast(U32).indirect(entries(offs_sb, a, b)))
@@ -143,23 +144,39 @@ def tile_picked_ringwsumdot_none_po_kernel(
             nc.vector.tensor_tensor(right[:, t, a:b], gained[t][:].indirect(entries(n2_sb, a, b)), sig3[:, t, a:b], MULT)
 
         def sum_z(a, b):
-            nc.vector.tensor_tensor(weave(z_bf, a, b, 4), planes(left, a, b, 4), planes(right, a, b, 4), ADD)
+            nc.vector.tensor_tensor(weave(z_bf, a, b, 2), planes(left, a, b, 2), planes(right, a, b, 2), ADD)
 
         def quantise_z(a, b):
             nc.vector.quantize_mx(z_codes[:, a:b].bitcast(FP8X4), z_scales[:, a:b], z_bf[:, PACK * a : PACK * b])
 
-        for t in range(PACK):
-            for a, b in HALVES if t == 0 else (WHOLE,):
-                bank = psum.tile([P, S], F32, name="bank")
-                product(bank[:, : b - a], t, x_codes[:, a:b], scales[:, H + a : H + b])
-                nc.scalar.activation(rows[t][:, a:b], bank[:, : b - a], COPY, scale=0.0625)
-                nc.scalar.activation(sig[:, t, a:b], bank[:, : b - a], SIGMOID, scale=0.0625)
-                nc.vector.tensor_scalar(gained[t][:, a:b], rows[t][:, a:b], gs_sb[:, t : t + 1], None, MULT)
-            for a, b in HALVES if t == LAST else (WHOLE,):
-                nc.scalar.activation(sig3[:, t, a:b], rows[t][:].indirect(entries(n3_sb, a, b)), SIGMOID)
-            if t < LAST:
-                first_term(t, *WHOLE)
-                second_term(t, *WHOLE)
+        def multiply_x(t, a, b):
+            bank = psum.tile([P, S], F32, name="bank")
+            product(bank[:, a:b], t, x_codes[:, a:b], scales[:, H + a : H + b])
+            nc.scalar.activation(rows[t][:, a:b], bank[:, a:b], COPY, scale=0.0625)
+            return bank
+
+        def gain(t, a, b):
+            nc.vector.tensor_scalar(gained[t][:, a:b], rows[t][:, a:b], gs_sb[:, t : t + 1], None, MULT)
+
+        def sigmoid(t, a, b, bank):
+            nc.scalar.activation(sig[:, t, a:b], bank[:, a:b], SIGMOID, scale=0.0625)
+
+        def sigmoid_at3(t, a, b):
+            nc.scalar.activation(sig3[:, t, a:b], rows[t][:].indirect(entries(n3_sb, a, b)), SIGMOID)
+
+        for a, b in HALVES:
+            bank = multiply_x(0, a, b)
+            sigmoid(0, a, b, bank)
+            gain(0, a, b)
+        for t in range(LAST):
+            first_term(t, *WHOLE)
+            bank = multiply_x(t + 1, *WHOLE)
+            gain(t + 1, *WHOLE)
+            sigmoid_at3(t, *WHOLE)
+            second_term(t, *WHOLE)
+            sigmoid(t + 1, *WHOLE, bank)
+        for a, b in HALVES:
+            sigmoid_at3(LAST, a, b)
         lo, hi = HALVES
         first_term(LAST, *lo)
         second_term(LAST, *lo)
@@ -238,7 +255,7 @@ def tile_picked_ringwsumdot_none_po_kernel(
         sum_y(LAST, *two)
         nc.scalar.copy(weave(y_bf, *two, 4), planes(y, *two, 4))
         terms(LAST, *three)
-        nc.vector.tensor_tensor(weave(y_bf, *three, 4), planes(term4, *three, 4), planes(term56, *three, 4), ADD)
+        nc.vector.tensor_tensor(weave(y_bf, *three, 2), planes(term4, *three, 2), planes(term56, *three, 2), ADD)
         sum_y(LAST, *three)
         quantise_y(*lo, nc.sync)
         quantise_y(*hi, nc.scalar)

@@ -249,11 +249,11 @@ def tile_picked_ringwsumdot_none_po_kernel(
         terms(LAST, *one)
         fetch5(LAST, *two)
         sum_y(LAST, *one)
-        nc.scalar.copy(weave(y_bf, *one, 4), planes(y, *one, 4))
+        nc.scalar.copy(weave(y_bf, *one, 2), planes(y, *one, 2))
         terms(LAST, *two)
         fetch5(LAST, *three)
         sum_y(LAST, *two)
-        nc.scalar.copy(weave(y_bf, *two, 4), planes(y, *two, 4))
+        nc.scalar.copy(weave(y_bf, *two, 2), planes(y, *two, 2))
         terms(LAST, *three)
         nc.vector.tensor_tensor(weave(y_bf, *three, 2), planes(term4, *three, 2), planes(term56, *three, 2), ADD)
         sum_y(LAST, *three)

import math
from contextlib import ExitStack

import concourse.mybir as mybir
from concourse.masks import make_identity

K, T, S, G, H = 512, 2048, 512, 2048, 512
FLOPS = 2 * 2 * K * H * S

F32 = mybir.dt.float32
BF16 = mybir.dt.bfloat16
I32 = mybir.dt.int32
U32 = mybir.dt.uint32
U16 = mybir.dt.uint16
U8 = mybir.dt.uint8
FP8X4 = mybir.dt.float8_e4m3fn_x4
MULT = mybir.AluOpType.mult
ADD = mybir.AluOpType.add
COPY = mybir.ActivationFunctionType.Copy
SIGMOID = mybir.ActivationFunctionType.Sigmoid

P = 128
PACK = 4
LAST = PACK - 1
FIRST = 512
WHOLE = (0, S)
HALVES = ((0, 256), (256, 512))
PIECES = ((0, 256), (256, 384), (384, 512))


def entries(lst, a, b):
    return lst[:, a // 16 : b // 16]


def words_of(packed):
    return packed[0].rearrange("p n t -> p (n t)").bitcast(I32)


def tile_picked_ringwsumdot_none_po_kernel(
    tc, x_words, x_scales, d_words, d_scales, gs, offs, k1, n1, n2, n3, n4, n5, n6, out_0, out_1, out_2
):
    nc = tc.nc
    with ExitStack() as ctx:
        keep = ctx.enter_context(tc.tile_pool(name="keep", bufs=1))
        psum = ctx.enter_context(tc.psum_pool(name="psum", bufs=8))

        def sb(name, shape, dtype):
            return keep.tile(shape, dtype, name=name, align_bytes=64)

        def load_list(name, src):
            lst = sb(name, [P, S // 16], U16)
            nc.sync.dma_start(lst[:], src)
            return lst

        d_byte_table = sb("d_byte_table", [P, G], U8)
        x_byte_table = sb("x_byte_table", [P, T], U8)
        d_word_table = sb("d_word_table", [P, G], I32)
        x_word_table = sb("x_word_table", [P, T], I32)
        nc.gpsimd.memset(d_byte_table[:].bitcast(I32), 0)
        nc.vector.memset(x_byte_table[:].bitcast(I32), 0)
        k1_sb = load_list("k1_sb", k1)
        nc.sync.dma_start(d_word_table[:, :FIRST], words_of(d_words)[:, :FIRST])
        nc.sync.dma_start(d_byte_table[0:P:8, :].bitcast(I32), d_scales[0].bitcast(I32))
        offs_sb = load_list("offs_sb", offs)
        nc.sync.dma_start(x_byte_table[0:P:8, :].bitcast(I32), x_scales[0].bitcast(I32))
        nc.sync.dma_start(d_word_table[:, FIRST:], words_of(d_words)[:, FIRST:])
        nc.sync.dma_start(x_word_table[:], words_of(x_words))
        gs_sb = sb("gs_sb", [P, PACK], F32)
        nc.sync.dma_start(gs_sb[:], gs.rearrange("(p t) o -> p (t o)", t=PACK))
        n1_sb = load_list("n1_sb", n1)
        n3_sb = load_list("n3_sb", n3)
        n2_sb = load_list("n2_sb", n2)
        n5_sb = load_list("n5_sb", n5)
        n4_sb = load_list("n4_sb", n4)
        n6_sb = load_list("n6_sb", n6)

        scales = sb("scales", [P, H + S], U8)
        nc.vector.memset(scales[:].bitcast(I32), 0)

        rows = [sb("rows%d" % t, [P, S if t == LAST else 2 * S], F32) for t in range(PACK)]
        gained = [sb("gained%d" % t, [P, S if t == LAST else 2 * S], F32) for t in range(PACK)]

        ident = sb("ident", [P, P], F32)
        make_identity(nc, ident[:])
        zero = sb("zero", [P, 1], F32)
        nc.vector.memset(zero[:], 0.0)

        d_bytes = sb("d_bytes", [P, H], U8)
        x_bytes = sb("x_bytes", [P, S], U8)
        spread = sb("spread", [P, H + S], U8)
        nc.vector.tensor_copy(d_bytes[:], d_byte_table[:].indirect(k1_sb[:]))
        nc.vector.tensor_copy(x_bytes[:], x_byte_table[:].indirect(offs_sb[:]))
        nc.vector.tensor_copy(
            spread[:, :H].rearrange("p (t m) -> p t m", t=PACK), d_bytes[:].rearrange("p (m t) -> p t m", t=PACK)
        )
        nc.vector.tensor_copy(spread[:, H:].bitcast(I32), x_bytes[:].bitcast(I32))
        for j in range(PACK):
            nc.scalar.dma_start(scales[j:P:32, :].bitcast(I32), spread[8 * j : P : 32, :].bitcast(I32))

        for t in range(LAST):
            for window in (gained[t], rows[t]):
                nc.scalar.activation(window[:, S:], zero[:].to_broadcast([P, S]), SIGMOID)

        d_picked = sb("d_picked", [P, H], U32)
        d_codes = sb("d_codes", [P, H], U32)
        x_codes = sb("x_codes", [P, S], U32)
        nc.vector.tensor_copy(d_picked[:], d_word_table[:].bitcast(U32).indirect(k1_sb[:]))
        nc.vector.tensor_copy(
            d_codes[:].bitcast(I32).rearrange("p (t c i) -> p c t i", t=PACK, i=4),
            d_picked[:].bitcast(I32).rearrange("p (c i t) -> p c t i", t=PACK, i=4),
        )
        for a, b in HALVES:
            nc.vector.tensor_copy(x_codes[:, a:b], x_word_table[:].bitcast(U32).indirect(entries(offs_sb, a, b)))

        def product(out, t, codes, codes_scale):
            nc.tensor.matmul_mx(
                out,
                lhsT=d_codes[:, t * P : (t + 1) * P].bitcast(FP8X4),
                lhsT_scale=scales[:, t * P : (t + 1) * P],
                rhs=codes.bitcast(FP8X4),
                rhs_scale=codes_scale,
                start=True,
                stop=True,
            )

        sig = sb("sig", [P, PACK, S], F32)
        sig3 = sb("sig3", [P, PACK, S], F32)
        left = sb("left", [P, PACK, S], F32)
        right = sb("right", [P, PACK, S], F32)
        z_bf = sb("z_bf", [P, S * PACK], BF16)
        z_codes = sb("z_codes", [P, S], U32)
        z_scales = sb("z_scales", [P, S], U8)

        def weave(dst, a, b, i):
            return dst[:, PACK * a : PACK * b].rearrange("p (c i t) -> p c t i", i=i, t=PACK)

        def planes(src, a, b, i):
            return src[:, :, a:b].rearrange("p t (c i) -> p c t i", i=i)

        def first_term(t, a, b):
            nc.vector.tensor_tensor(left[:, t, a:b], gained[t][:].indirect(entries(n1_sb, a, b)), sig[:, t, a:b], MULT)

        def second_term(t, a, b):
            nc.vector.tensor_tensor(right[:, t, a:b], gained[t][:].indirect(entries(n2_sb, a, b)), sig3[:, t, a:b], MULT)

        def sum_z(a, b):
            nc.vector.tensor_tensor(weave(z_bf, a, b, 2), planes(left, a, b, 2), planes(right, a, b, 2), ADD)

        def quantise_z(a, b):
            nc.vector.quantize_mx(z_codes[:, a:b].bitcast(FP8X4), z_scales[:, a:b], z_bf[:, PACK * a : PACK * b])

        def multiply_x(t, a, b):
            bank = psum.tile([P, S], F32, name="bank")
            product(bank[:, a:b], t, x_codes[:, a:b], scales[:, H + a : H + b])
            nc.scalar.activation(rows[t][:, a:b], bank[:, a:b], COPY, scale=0.0625)
            return bank

        def gain(t, a, b):
            nc.vector.tensor_scalar(gained[t][:, a:b], rows[t][:, a:b], gs_sb[:, t : t + 1], None, MULT)

        def sigmoid(t, a, b, bank):
            nc.scalar.activation(sig[:, t, a:b], bank[:, a:b], SIGMOID, scale=0.0625)

        def sigmoid_at3(t, a, b):
            nc.scalar.activation(sig3[:, t, a:b], rows[t][:].indirect(entries(n3_sb, a, b)), SIGMOID)

        for a, b in HALVES:
            bank = multiply_x(0, a, b)
            sigmoid(0, a, b, bank)
            gain(0, a, b)
        for t in range(LAST):
            first_term(t, *WHOLE)
            bank = multiply_x(t + 1, *WHOLE)
            gain(t + 1, *WHOLE)
            sigmoid_at3(t, *WHOLE)
            second_term(t, *WHOLE)
            sigmoid(t + 1, *WHOLE, bank)
        for a, b in HALVES:
            sigmoid_at3(LAST, a, b)
        lo, hi = HALVES
        first_term(LAST, *lo)
        second_term(LAST, *lo)
        first_term(LAST, *hi)
        sum_z(*lo)
        second_term(LAST, *hi)
        quantise_z(*lo)
        sum_z(*hi)
        quantise_z(*hi)

        root = 0.0625 * math.sqrt(0.75)
        plain = sb("plain", [P, PACK, S], F32)
        at5 = sb("at5", [P, PACK, S], F32)
        term4 = sb("term4", [P, PACK, S], F32)
        term56 = sb("term56", [P, PACK, S], F32)
        y = sb("y", [P, PACK, S], F32)
        y_turned = sb("y_turned", [P, 2, S], F32)
        y_bf = sb("y_bf", [P, S * PACK], BF16)
        y_codes = sb("y_codes", [P, S], U32)
        y_scales = sb("y_scales", [P, S], U8)
        out_rows = out_0.rearrange("(p t) n -> p t n", t=PACK)
        out_words = words_of(out_1)

        def fetch5(t, a, b):
            nc.vector.tensor_copy(at5[:, t, a:b], rows[t][:].indirect(entries(n5_sb, a, b)))

        def terms(t, a, b):
            nc.vector.tensor_tensor(term4[:, t, a:b], rows[t][:].indirect(entries(n4_sb, a, b)), plain[:, t, a:b], MULT)
            nc.vector.tensor_tensor(term56[:, t, a:b], rows[t][:].indirect(entries(n6_sb, a, b)), at5[:, t, a:b], MULT)

        def sum_y(t, a, b):
            nc.vector.tensor_tensor(y[:, t, a:b], term4[:, t, a:b], term56[:, t, a:b], ADD)
            nc.sync.dma_start(out_rows[:, t, a:b], y[:, t, a:b])

        def sum_y_by_transposes(t):
            turned = psum.tile([P, S], F32, name="bank")
            for c in range(0, S, P):
                for src, first in ((term4, True), (term56, False)):
                    nc.tensor.matmul(
                        turned[:, c : c + P], lhsT=src[:, t, c : c + P], rhs=ident[:], is_transpose=True, start=first, stop=not first
                    )
            nc.scalar.copy(y_turned[:, t, :], turned[:])
            back = psum.tile([P, S], F32, name="bank")
            for c in range(0, S, P):
                nc.tensor.transpose(back[:, c : c + P], y_turned[:, t, c : c + P], ident[:])
            nc.scalar.copy(y[:, t, :], back[:])
            nc.scalar.dma_start(out_rows[:, t, :], y[:, t, :])

        def quantise_y(a, b, queue):
            nc.vector.quantize_mx(y_codes[:, a:b].bitcast(FP8X4), y_scales[:, a:b], y_bf[:, PACK * a : PACK * b])
            queue.dma_start(out_words[:, a:b], y_codes[:, a:b].bitcast(I32))

        for t in range(PACK):
            banks = []
            for a, b in HALVES if t == 0 else (WHOLE,):
                bank = psum.tile([P, S], F32, name="bank")
                product(bank[:, a:b], t, z_codes[:, a:b], z_scales[:, a:b])
                nc.scalar.activation(rows[t][:, a:b], bank[:, a:b], COPY, scale=root)
                banks.append((a, b, bank))
            for a, b, bank in banks:
                nc.scalar.activation(plain[:, t, a:b], bank[:, a:b], COPY, scale=root)
            if t < LAST:
                fetch5(t, *WHOLE)
                terms(t, *WHOLE)
        for t in range(2):
            sum_y_by_transposes(t)
        one, two, three = PIECES
        fetch5(LAST, *one)
        sum_y(LAST - 1, *WHOLE)
        terms(LAST, *one)
        fetch5(LAST, *two)
        sum_y(LAST, *one)
        nc.scalar.copy(weave(y_bf, *one, 2), planes(y, *one, 2))
        terms(LAST, *two)
        fetch5(LAST, *three)
        sum_y(LAST, *two)
        nc.scalar.copy(weave(y_bf, *two, 2), planes(y, *two, 2))
        terms(LAST, *three)
        nc.vector.tensor_tensor(weave(y_bf, *three, 2), planes(term4, *three, 2), planes(term56, *three, 2), ADD)
        sum_y(LAST, *three)
        quantise_y(*lo, nc.sync)
        quantise_y(*hi, nc.scalar)
        for q in range(4):
            queue = nc.sync if q < 2 else nc.scalar
            queue.dma_start(out_2[0, 4 * q : 4 * q + 4, :].bitcast(I32), y_scales[32 * q : 32 * q + 4, :].bitcast(I32))
